import numpy as np
import ml_dtypes


def mxq(x, axis, fmt="e4m3"):
    dtype, down = {"e4m3": (ml_dtypes.float8_e4m3fn, 7), "e5m2": (ml_dtypes.float8_e5m2, 14)}[fmt]
    v = np.moveaxis(np.asarray(x, np.float32).astype(ml_dtypes.bfloat16).astype(np.float64), axis, -1)
    blocks = v.reshape(v.shape[:-1] + (-1, 32))
    amax = np.abs(blocks).max(-1, keepdims=True)
    byte = np.maximum(np.where(amax > 0, np.frexp(amax)[1] - 1 + 127, 0) - down, 1)
    scale = np.exp2(byte - 127.0)
    codes = (blocks / scale).astype(np.float32).astype(dtype).astype(np.float64)
    return np.moveaxis((codes * scale).reshape(v.shape), -1, axis)


WIDE = False


def mx_kscale(k):
    if not WIDE:
        return np.ones(k)
    levels = np.array([10, -10, 5, -5, 0])
    if k % 512:
        return np.exp2(np.random.permutation(np.resize(levels, k // 32))).repeat(32)
    a = np.empty((k // 512, 16))
    for p in range(k // 512):
        a[p, :8] = np.random.permutation(np.resize(levels, 8))
        for g in range(8):
            far = levels[np.abs(levels - a[p, g]) >= 10]
            a[p, g + 8] = far[np.random.randint(len(far))]
    return np.exp2(a.ravel()).repeat(32)


def f64(x):
    return np.asarray(x).astype(np.float64)


def striped(idx):
    return np.tile(idx.reshape(-1, 16).T, (8, 1)).astype(np.uint16)


def unstriped(offs):
    return offs[:16].T.reshape(-1).astype(np.int64)


def striped8(idx):
    return np.concatenate([x.reshape(-1, 16).T for x in idx]).astype(np.uint16)


def runs(offs, k):
    lists = np.stack([offs[16 * r : 16 * r + 16].T.reshape(-1) for r in range(8)]).astype(np.int64)
    return lists[np.arange(k) % 512 // 64]


def pack_weight(w):
    k, n = w.shape
    w = f64(np.asarray(w, np.float32).astype(ml_dtypes.bfloat16)).reshape(k // 32, 32, n)
    amax = np.abs(w).max(1)
    byte = np.clip(np.where(amax > 0, np.frexp(amax)[1] - 1 + 127 - 7, 1), 1, 254)
    scaled = (w * np.exp2(127.0 - byte)[:, None, :]).reshape(k, n).astype(np.float32)
    words = np.ascontiguousarray(scaled.reshape(k // 512, 128, 4, n).transpose(0, 1, 3, 2)).astype(ml_dtypes.float8_e4m3fn).view(np.uint8)
    return words, np.ascontiguousarray(byte.astype(np.uint8).reshape(k // 512, 16, n))


def unpack_weight(words, scales):
    g, p, n, _ = words.shape
    vals = np.ascontiguousarray(words).view(ml_dtypes.float8_e4m3fn).astype(np.float64) * np.repeat(np.exp2(scales.astype(np.float64) - 127.0), 8, axis=1)[..., None]
    return vals.transpose(0, 1, 3, 2).reshape(g * 512, n)


def relu(v):
    return np.maximum(v, 0.0)

def planes(y):
    n, m = y.shape
    v = y.astype(np.float32).astype(ml_dtypes.bfloat16).astype(np.float64).reshape(n // 32, 32, m)
    top = np.abs(v).max(1)
    byte = np.clip(np.where(top > 0, np.frexp(top)[1] - 1 + 127 - 7, 1), 1, 254)
    codes = (v * np.exp2(127.0 - byte)[:, None, :]).reshape(n, m).astype(np.float32).astype(ml_dtypes.float8_e4m3fn).view(np.uint8)
    words = codes.reshape(n // 512, 128, 4, m).transpose(0, 1, 3, 2)
    return np.ascontiguousarray(words), np.ascontiguousarray(byte.astype(np.uint8).reshape(n // 512, 16, m))


K, T, S, N, H, U = 512, 2048, 512, 512, 512, 1024


def setup_inputs():
    n = np.random.standard_normal
    s = mx_kscale(K)[:, None]
    u = mx_kscale(S)
    packed_xT = pack_weight(n((K, T)) * s)
    packed_w1 = pack_weight(n((S, N)) / np.sqrt(S) / u[:, None])
    return {
        "x_words": packed_xT[0],
        "x_scales": packed_xT[1],
        "wa": (n((K, H)) / np.sqrt(K) / s).astype(np.float32),
        "wb": (n((K, H)) / np.sqrt(K) / s).astype(np.float32),
        "gt": (np.random.uniform(0.5, 1.5, (S, 1)) * u[:, None]).astype(np.float32),
        "w1_words": packed_w1[0],
        "w1_scales": packed_w1[1],
        "offs": striped(np.random.permutation(T)[:S]),
        "two": striped(np.random.permutation(T)[:S]),
        "n1": striped8(np.stack([np.random.permutation(H) for _ in range(8)])),
        "n2": striped8(np.stack([np.random.permutation(H) for _ in range(8)])),
        "n3": striped8(np.stack([np.random.permutation(U)[:H] for _ in range(8)])),
        "n4": striped8(np.stack([np.random.permutation(H) for _ in range(8)])),
    }


def reference(x_words, x_scales, wa, wb, gt, w1_words, w1_scales, offs, two, n1, n2, n3, n4):
    xq = unpack_weight(x_words, x_scales)[:, unstriped(offs)]
    y = xq.T @ mxq(f64(wa), 0, "e4m3")
    x_two = unpack_weight(x_words, x_scales)[:, unstriped(two)]
    d = x_two.T @ mxq(f64(wb), 0, "e4m3")
    z = f64(gt) * (y * (np.tanh(d[np.arange(S)[:, None], runs(n1, S)] - (d[np.arange(S)[:, None], runs(n2, S)]))))
    h = unpack_weight(w1_words, w1_scales).T @ mxq(z, 0, "e4m3")
    nw = h - (relu(h[np.arange(N)[:, None], runs(n4, N)]))
    out = np.zeros((N, U))
    out[np.arange(N)[:, None], runs(n3, N)] = nw
    return (out,) + planes(out)

@@ -1,0 +1,275 @@
+from contextlib import ExitStack
+
+import concourse.mybir as mybir
+
+K, T, S, N, H, U = 512, 2048, 512, 512, 512, 1024
+FLOPS = 2 * K * S * H * 2 + 2 * S * N * H
+
+F32 = mybir.dt.float32
+BF16 = mybir.dt.bfloat16
+I32 = mybir.dt.int32
+U32 = mybir.dt.uint32
+U16 = mybir.dt.uint16
+U8 = mybir.dt.uint8
+FP8X4 = mybir.dt.float8_e4m3fn_x4
+ALU = mybir.AluOpType
+ACT = mybir.ActivationFunctionType
+
+P = 128
+PACK = 4
+HALF = 256
+WIDE = 1024
+
+
+def tile_picked_twtjointbpagez_none_po_kernel(
+    tc, x_words, x_scales, wa, wb, gt, w1_words, w1_scales, offs, two, n1, n2, n3, n4, out_0, out_1, out_2
+):
+    nc = tc.nc
+    with ExitStack() as ctx:
+        lists = ctx.enter_context(tc.tile_pool(name="lists", bufs=1))
+        keep = ctx.enter_context(tc.tile_pool(name="keep", bufs=1))
+        psum = ctx.enter_context(tc.psum_pool(name="psum", bufs=8))
+
+        def sb(name, shape, dtype, tag=None):
+            return keep.tile(shape, dtype, name=name, tag=tag or name, align_bytes=64)
+
+        def bank():
+            return psum.tile([P, 512], F32, name="bank")
+
+        def load_list(name, src):
+            tile = lists.tile([P, 32], U16, name=name)
+            nc.sync.dma_start(tile[:], src)
+            return tile
+
+        def load_scale_rows(queue, tile, src):
+            for q in range(4):
+                queue.dma_start(tile[32 * q : 32 * q + 4, :].bitcast(I32), src[0, 4 * q : 4 * q + 4, :].bitcast(I32))
+
+        def words_view(src):
+            return src[0].rearrange("p c r -> p (c r)").bitcast(I32)
+
+        def deal_words(dst, src):
+            nc.vector.tensor_copy(
+                dst[:].rearrange("p (t c i) -> p c t i", t=PACK, i=4),
+                src[:].rearrange("p (c i t) -> p c t i", t=PACK, i=4),
+            )
+
+        def deal_bytes(dst, src):
+            nc.vector.tensor_copy(
+                dst[:].rearrange("p (t c i) -> p c t i", t=PACK, i=16),
+                src[:].rearrange("p (c i t) -> p c t i", t=PACK, i=16),
+            )
+
+        def mx(acc, lhs, lhs_scale, t, rhs, rhs_scale, cols):
+            rows = slice(P * t, P * (t + 1))
+            nc.tensor.matmul_mx(
+                out=acc, lhsT=lhs[:, rows].bitcast(FP8X4), lhsT_scale=lhs_scale[:, rows],
+                rhs=rhs[:, cols].bitcast(FP8X4), rhs_scale=rhs_scale[:, cols], start=True, stop=True,
+            )
+
+        xs = sb("xs", [P, T], U8)
+        nc.gpsimd.memset(xs[:].bitcast(I32), 0)
+        load_scale_rows(nc.scalar, xs, x_scales)
+        two_l = load_list("two_l", two)
+        offs_l = load_list("offs_l", offs)
+        n2_l = load_list("n2_l", n2)
+        n1_l = load_list("n1_l", n1)
+        xw = sb("xw", [P, T], U32)
+        nc.sync.dma_start(xw[:].bitcast(I32), words_view(x_words))
+
+        def load_weight_half(name, w, u):
+            raw = sb(name, [P, PACK, HALF], F32)
+            nc.sync.dma_start(raw[:], w.rearrange("(p j) c -> p j c", j=PACK)[:, :, HALF * u : HALF * (u + 1)])
+            return raw
+
+        wb_raw = [load_weight_half("wb_raw%d" % u, wb, u) for u in range(2)]
+        wa_raw = [load_weight_half("wa_raw%d" % u, wa, u) for u in range(2)]
+        w1s = sb("w1s", [P, N], U8)
+        nc.gpsimd.memset(w1s[:].bitcast(I32), 0)
+        w1w = sb("w1w", [P, N], U32)
+        nc.sync.dma_start(w1w[:].bitcast(I32), words_view(w1_words))
+        load_scale_rows(nc.sync, w1s, w1_scales)
+        gate = sb("gate", [P, PACK], F32)
+        nc.sync.dma_start(gate[:], gt.rearrange("(p t) o -> p (t o)", t=PACK))
+        n4_l = load_list("n4_l", n4)
+        n3_l = load_list("n3_l", n3)
+
+        pages = [sb("page%d" % t, [P, U], F32) for t in range(PACK)]
+        for t in range(PACK):
+            nc.vector.memset(pages[t][:], 0.0)
+
+        def pick_bytes(name, lst):
+            got = sb(name + "_got", [P, S], U8)
+            nc.vector.tensor_copy(got[:], xs[:].indirect(lst[:]))
+            return got
+
+        def pick_words(name, lst, tag=None):
+            got = sb(name + "_got", [P, S], U32, tag)
+            nc.vector.tensor_copy(got[:], xw[:].indirect(lst[:]))
+            return got
+
+        bw_got = pick_words("bw", two_l)
+        bs_got = pick_bytes("bs", two_l)
+        b_words = sb("b_words", [P, S], U32)
+        deal_words(b_words, bw_got)
+        b_scale = sb("b_scale", [P, S], U8)
+        deal_bytes(b_scale, bs_got)
+        as_got = pick_bytes("as", offs_l)
+
+        def round_weight_half(name, raw):
+            grouped = sb(name, [P, HALF, PACK], BF16)
+            nc.scalar.activation(
+                grouped[:].rearrange("p (c i) j -> p c j i", i=2),
+                raw[:].rearrange("p j (c i) -> p c j i", i=2), ACT.Copy,
+            )
+            return grouped
+
+        def quantise(codes, scales, cols, grouped):
+            nc.vector.quantize_mx(
+                out=codes[:, cols].bitcast(FP8X4), scales=scales[:, cols], in_=grouped[:].rearrange("p c j -> p (c j)")
+            )
+
+        halves = [slice(0, HALF), slice(HALF, 2 * HALF)]
+        whole = slice(0, H)
+        wb_codes = sb("wb_codes", [P, H], U32)
+        wb_scale = sb("wb_scale", [P, H], U8)
+        for u in range(2):
+            quantise(wb_codes, wb_scale, halves[u], round_weight_half("wb_bf%d" % u, wb_raw[u]))
+        aw_got = pick_words("aw", offs_l, "wb_bf1")
+        a_scale = sb("a_scale", [P, S], U8)
+        deal_bytes(a_scale, as_got)
+        a_words = sb("a_words", [P, S], U32)
+        deal_words(a_words, aw_got)
+
+        d_rows = [sb("d%d" % t, [P, H], F32) for t in range(PACK)]
+
+        def project_d(t, cols):
+            acc = bank()
+            mx(acc[:, cols], b_words, b_scale, t, wb_codes, wb_scale, cols)
+            nc.scalar.copy(d_rows[t][:, cols], acc[:, cols])
+
+        wa_codes = sb("wa_codes", [P, H], U32)
+        wa_scale = sb("wa_scale", [P, H], U8)
+        project_d(0, halves[0])
+        project_d(0, halves[1])
+        project_d(1, whole)
+        wa_bf = [round_weight_half("wa_bf%d" % u, wa_raw[u]) for u in range(2)]
+        project_d(2, whole)
+        project_d(3, whole)
+
+        yg = sb("yg", [P, PACK, H], F32)
+
+        def entries(lst, cols):
+            return lst[:, cols.start // 16 : cols.stop // 16]
+
+        def fetch_diff(t, tag=None):
+            second = [sb("second%d_%d" % (t, u), [P, HALF], F32, tag if u == 0 else None) for u in range(2)]
+            diff = [sb("diff%d_%d" % (t, u), [P, HALF], F32) for u in range(2)]
+            for u in range(2):
+                nc.vector.tensor_copy(second[u][:], d_rows[t][:].indirect(entries(n2_l, halves[u])))
+            for u in range(2):
+                nc.vector.tensor_tensor(
+                    diff[u][:], d_rows[t][:].indirect(entries(n1_l, halves[u])), second[u][:], ALU.subtract
+                )
+            return diff
+
+        diffs = [fetch_diff(0), fetch_diff(1)]
+        for u in range(2):
+            quantise(wa_codes, wa_scale, halves[u], wa_bf[u])
+        for t in range(PACK):
+            acc = bank()
+            mx(acc[:], a_words, a_scale, t, wa_codes, wa_scale, whole)
+            nc.scalar.activation(yg[:, t, :], acc[:], ACT.Copy, scale=gate[:, t : t + 1])
+        diffs.append(fetch_diff(2, "wa_bf1"))
+        diffs.append(fetch_diff(3))
+        th = [sb("th0", [P, PACK, HALF], F32, "a_words"), sb("th1", [P, PACK, HALF], F32, "wa_codes")]
+        for t in range(PACK):
+            for u in range(2):
+                nc.scalar.activation(th[u][:, t, :], diffs[t][u][:], ACT.Tanh)
+
+        w1_dealt = sb("w1_dealt", [P, N], U32)
+        w1_scale = sb("w1_scale", [P, N], U8)
+        deal_words(w1_dealt, w1w)
+        deal_bytes(w1_scale, w1s)
+
+        pieces = [slice(0, 256), slice(256, 384), slice(384, 512)]
+        z_codes = sb("z_codes", [P, H], U32)
+        z_scale = sb("z_scale", [P, H], U8)
+        z_bf = [sb("z_bf%d" % k, [P, c.stop - c.start, PACK], BF16) for k, c in enumerate(pieces)]
+
+        def product(k):
+            cols = pieces[k]
+            u = cols.start // HALF
+            inner = slice(cols.start - HALF * u, cols.stop - HALF * u)
+            nc.vector.tensor_tensor(
+                z_bf[k][:].rearrange("p (c i) t -> p c t i", i=2),
+                yg[:, :, cols].rearrange("p t (c i) -> p c t i", i=2),
+                th[u][:, :, inner].rearrange("p t (c i) -> p c t i", i=2),
+                ALU.mult,
+            )
+
+        product(0)
+        product(1)
+        quantise(z_codes, z_scale, pieces[0], z_bf[0])
+        product(2)
+        quantise(z_codes, z_scale, pieces[1], z_bf[1])
+        quantise(z_codes, z_scale, pieces[2], z_bf[2])
+
+        pos = [sb("pos%d" % t, [P, WIDE], F32) for t in range(PACK)]
+        h_rows = [sb("h%d" % t, [P, H], F32) for t in range(PACK)]
+        waiting = []
+        for t in range(PACK):
+            made = []
+            for cols in (pieces if t == 0 else [whole]):
+                acc = bank()
+                mx(acc[:, cols], w1_dealt, w1_scale, t, z_codes, z_scale, cols)
+                nc.scalar.activation(pos[t][:, cols], acc[:, cols], ACT.Relu)
+                made.append((h_rows[t][:, cols], acc[:, cols]))
+            for dst, src in waiting:
+                nc.scalar.copy(dst, src)
+            waiting = made
+        for dst, src in waiting:
+            nc.scalar.copy(dst, src)
+
+        minus = [sb("minus%d" % t, [P, H], F32) for t in range(PACK)]
+        QUARTER = U // 4
+        quarters = [slice(QUARTER * k, QUARTER * (k + 1)) for k in range(4)]
+        page_bf = [sb("page_bf%d" % k, [P, QUARTER, PACK], BF16) for k in range(4)]
+        out_rows = out_0.rearrange("(p t) c -> p t c", t=PACK)
+
+        def fetch_minus(t):
+            nc.vector.tensor_scalar(minus[t][:], pos[t][:].indirect(n4_l[:]), -1.0, 0.0, ALU.mult, ALU.add)
+
+        def put(t):
+            nc.vector.tensor_tensor(pages[t][:].indirect(n3_l[:]), h_rows[t][:], minus[t][:], ALU.add)
+            nc.sync.dma_start(out_rows[:, t, :], pages[t][:])
+
+        def round_page(t, k, copy):
+            copy(page_bf[k][:, :, t], pages[t][:, quarters[k]])
+
+        fetch_minus(0)
+        fetch_minus(1)
+        for t in range(PACK - 1):
+            put(t)
+            for k in range(4):
+                if t == PACK - 2 and k < 2:
+                    nc.scalar.copy(page_bf[k][:, :, t:], pages[t][:, quarters[k]].unsqueeze(2).to_broadcast([P, QUARTER, 2]))
+                else:
+                    round_page(t, k, nc.scalar.copy)
+            if t + 2 < PACK:
+                fetch_minus(t + 2)
+        put(PACK - 1)
+        out_codes = sb("out_codes", [P, U], U32)
+        out_scale = sb("out_scale", [P, U], U8)
+        round_page(PACK - 1, 0, nc.vector.tensor_copy)
+        round_page(PACK - 1, 1, nc.vector.tensor_copy)
+        round_page(PACK - 1, 2, nc.scalar.copy)
+        round_page(PACK - 1, 3, nc.scalar.copy)
+        for k in range(4):
+            quantise(out_codes, out_scale, quarters[k], page_bf[k])
+            if k % 2 == 1:
+                cols = slice(quarters[k - 1].start, quarters[k].stop)
+                nc.sync.dma_start(words_view(out_1)[:, cols], out_codes[:, cols].bitcast(I32))
+        for q in range(4):
+            queue = nc.sync if q % 2 == 0 else nc.scalar
+            queue.dma_start(out_2[0, 4 * q : 4 * q + 4, :].bitcast(I32), out_scale[32 * q : 32 * q + 4, :].bitcast(I32))

@@ -68,12 +68,12 @@ def tile_picked_twtjointbpagez_none_po_kernel(
             )
 
         xs = sb("xs", [P, T], U8)
-        nc.gpsimd.memset(xs[:].bitcast(I32), 0)
-        load_scale_rows(nc.scalar, xs, x_scales)
+        nc.vector.memset(xs[:, : T // 2].bitcast(I32), 0)
+        nc.gpsimd.memset(xs[:, T // 2 :].bitcast(I32), 0)
+        load_scale_rows(nc.sync, xs, x_scales)
         two_l = load_list("two_l", two)
         offs_l = load_list("offs_l", offs)
         n2_l = load_list("n2_l", n2)
-        n1_l = load_list("n1_l", n1)
         xw = sb("xw", [P, T], U32)
         nc.sync.dma_start(xw[:].bitcast(I32), words_view(x_words))
 
@@ -83,7 +83,10 @@ def tile_picked_twtjointbpagez_none_po_kernel(
             return raw
 
         wb_raw = [load_weight_half("wb_raw%d" % u, wb, u) for u in range(2)]
-        wa_raw = [load_weight_half("wa_raw%d" % u, wa, u) for u in range(2)]
+        n1_l = load_list("n1_l", n1)
+        wa_all = sb("wa_all", [P, PACK, H], F32)
+        nc.sync.dma_start(wa_all[:], wa.rearrange("(p j) c -> p j c", j=PACK))
+        wa_raw = [wa_all[:, :, HALF * u : HALF * (u + 1)] for u in range(2)]
         w1s = sb("w1s", [P, N], U8)
         nc.gpsimd.memset(w1s[:].bitcast(I32), 0)
         w1w = sb("w1w", [P, N], U32)
@@ -94,33 +97,37 @@ def tile_picked_twtjointbpagez_none_po_kernel(
         n4_l = load_list("n4_l", n4)
         n3_l = load_list("n3_l", n3)
 
-        pages = [sb("page%d" % t, [P, U], F32) for t in range(PACK)]
-        for t in range(PACK):
-            nc.vector.memset(pages[t][:], 0.0)
+        pages = [sb("page%d" % t, [P, U], F32) for t in range(PACK - 1)]
+        for page in pages:
+            nc.vector.memset(page[:].bitcast(I32), 0)
+        pages.append(pages[0])
 
-        def pick_bytes(name, lst):
-            got = sb(name + "_got", [P, S], U8)
+        def pick_bytes(name, lst, tag):
+            got = sb(name + "_got", [P, S], U8, tag)
             nc.vector.tensor_copy(got[:], xs[:].indirect(lst[:]))
             return got
 
         def pick_words(name, lst, tag=None):
-            got = sb(name + "_got", [P, S], U32, tag)
-            nc.vector.tensor_copy(got[:], xw[:].indirect(lst[:]))
+            got = sb(name + "_got", [P, 16 * lst.shape[1]], U32, tag)
+            nc.vector.tensor_copy(got[:], xw[:].indirect(lst))
             return got
 
-        bw_got = pick_words("bw", two_l)
-        bs_got = pick_bytes("bs", two_l)
-        b_words = sb("b_words", [P, S], U32)
-        deal_words(b_words, bw_got)
+        bs_got = pick_bytes("bs", two_l, None)
+        as_got = pick_bytes("as", offs_l, None)
         b_scale = sb("b_scale", [P, S], U8)
         deal_bytes(b_scale, bs_got)
-        as_got = pick_bytes("as", offs_l)
+        bw_got = pick_words("bw", two_l[:])
+        aw_first = pick_words("aw0", offs_l[:, :16])
+        a_scale = sb("a_scale", [P, S], U8)
+        deal_bytes(a_scale, as_got)
+        b_words = sb("b_words", [P, S], U32)
+        deal_words(b_words, bw_got)
 
         def round_weight_half(name, raw):
             grouped = sb(name, [P, HALF, PACK], BF16)
             nc.scalar.activation(
-                grouped[:].rearrange("p (c i) j -> p c j i", i=2),
-                raw[:].rearrange("p j (c i) -> p c j i", i=2), ACT.Copy,
+                grouped[:].rearrange("p (c i) j -> p c j i", i=4),
+                raw.rearrange("p j (c i) -> p c j i", i=4), ACT.Copy,
             )
             return grouped
 
@@ -134,14 +141,16 @@ def tile_picked_twtjointbpagez_none_po_kernel(
         wb_codes = sb("wb_codes", [P, H], U32)
         wb_scale = sb("wb_scale", [P, H], U8)
         for u in range(2):
-            quantise(wb_codes, wb_scale, halves[u], round_weight_half("wb_bf%d" % u, wb_raw[u]))
-        aw_got = pick_words("aw", offs_l, "wb_bf1")
-        a_scale = sb("a_scale", [P, S], U8)
-        deal_bytes(a_scale, as_got)
+            quantise(wb_codes, wb_scale, halves[u], round_weight_half("wb_bf%d" % u, wb_raw[u][:]))
+        aw_second = pick_words("aw1", offs_l[:, 16:], "wb_bf1")
         a_words = sb("a_words", [P, S], U32)
-        deal_words(a_words, aw_got)
+        for u, got in enumerate((aw_first, aw_second)):
+            nc.vector.tensor_copy(
+                a_words[:].rearrange("p (t u c i) -> p u c t i", t=PACK, u=2, i=4)[:, u],
+                got[:].rearrange("p (c i t) -> p c t i", t=PACK, i=4),
+            )
 
-        d_rows = [sb("d%d" % t, [P, H], F32) for t in range(PACK)]
+        d_rows = [sb("d%d" % t, [P, WIDE], F32) for t in range(PACK)]
 
         def project_d(t, cols):
             acc = bank()
@@ -150,47 +159,60 @@ def tile_picked_twtjointbpagez_none_po_kernel(
 
         wa_codes = sb("wa_codes", [P, H], U32)
         wa_scale = sb("wa_scale", [P, H], U8)
-        project_d(0, halves[0])
-        project_d(0, halves[1])
-        project_d(1, whole)
+        for u in range(2):
+            for t in range(2):
+                project_d(t, halves[u])
         wa_bf = [round_weight_half("wa_bf%d" % u, wa_raw[u]) for u in range(2)]
         project_d(2, whole)
         project_d(3, whole)
 
         yg = sb("yg", [P, PACK, H], F32)
 
-        def entries(lst, cols):
-            return lst[:, cols.start // 16 : cols.stop // 16]
+        def fetch_second(t):
+            second = sb("second%d" % t, [P, H], F32)
+            nc.vector.tensor_copy(second[:], d_rows[t][:].indirect(n2_l[:]))
+            return second
 
-        def fetch_diff(t, tag=None):
-            second = [sb("second%d_%d" % (t, u), [P, HALF], F32, tag if u == 0 else None) for u in range(2)]
-            diff = [sb("diff%d_%d" % (t, u), [P, HALF], F32) for u in range(2)]
-            for u in range(2):
-                nc.vector.tensor_copy(second[u][:], d_rows[t][:].indirect(entries(n2_l, halves[u])))
-            for u in range(2):
+        def fetch_diff(t, second, parts, tag=None):
+            diff = sb("diff%d" % t, [P, H], F32, tag)
+            for cols in parts:
                 nc.vector.tensor_tensor(
-                    diff[u][:], d_rows[t][:].indirect(entries(n1_l, halves[u])), second[u][:], ALU.subtract
+                    diff[:, cols], d_rows[t][:].indirect(n1_l[:, cols.start // 16 : cols.stop // 16]),
+                    second[:, cols], ALU.subtract,
                 )
             return diff
 
-        diffs = [fetch_diff(0), fetch_diff(1)]
+        seconds = [fetch_second(0), fetch_second(1)]
+        diffs = [fetch_diff(0, seconds[0], [whole])]
         for u in range(2):
             quantise(wa_codes, wa_scale, halves[u], wa_bf[u])
         for t in range(PACK):
             acc = bank()
             mx(acc[:], a_words, a_scale, t, wa_codes, wa_scale, whole)
             nc.scalar.activation(yg[:, t, :], acc[:], ACT.Copy, scale=gate[:, t : t + 1])
-        diffs.append(fetch_diff(2, "wa_bf1"))
-        diffs.append(fetch_diff(3))
+        diffs.append(fetch_diff(1, seconds[1], [whole], "wa_bf1"))
+        seconds.extend([fetch_second(2), fetch_second(3)])
+        diffs.append(fetch_diff(2, seconds[2], [whole]))
+        diffs.append(fetch_diff(3, seconds[3], halves))
         th = [sb("th0", [P, PACK, HALF], F32, "a_words"), sb("th1", [P, PACK, HALF], F32, "wa_codes")]
         for t in range(PACK):
             for u in range(2):
-                nc.scalar.activation(th[u][:, t, :], diffs[t][u][:], ACT.Tanh)
+                nc.scalar.activation(th[u][:, t, :], diffs[t][:, halves[u]], ACT.Tanh)
 
-        w1_dealt = sb("w1_dealt", [P, N], U32)
-        w1_scale = sb("w1_scale", [P, N], U8)
-        deal_words(w1_dealt, w1w)
-        deal_bytes(w1_scale, w1s)
+        def deal_w1(name, first, count, tags):
+            words = sb(name + "_words", [P, count * P], U32, tags[0])
+            scale = sb(name + "_scale", [P, count * P], U8, tags[1])
+            nc.vector.tensor_copy(
+                words[:].rearrange("p (t c i) -> p c t i", t=count, i=4),
+                w1w[:].rearrange("p (c i t) -> p c t i", t=PACK, i=4)[:, :, first : first + count, :],
+            )
+            nc.vector.tensor_copy(
+                scale[:].rearrange("p (t c i) -> p c t i", t=count, i=16),
+                w1s[:].rearrange("p (c i t) -> p c t i", t=PACK, i=16)[:, :, first : first + count, :],
+            )
+            return words, scale
+
+        w1_dealt = [deal_w1("w1_early", 0, 1, (None, None))]
 
         pieces = [slice(0, 256), slice(256, 384), slice(384, 512)]
         z_codes = sb("z_codes", [P, H], U32)
@@ -202,9 +224,9 @@ def tile_picked_twtjointbpagez_none_po_kernel(
             u = cols.start // HALF
             inner = slice(cols.start - HALF * u, cols.stop - HALF * u)
             nc.vector.tensor_tensor(
-                z_bf[k][:].rearrange("p (c i) t -> p c t i", i=2),
-                yg[:, :, cols].rearrange("p t (c i) -> p c t i", i=2),
-                th[u][:, :, inner].rearrange("p t (c i) -> p c t i", i=2),
+                z_bf[k][:].rearrange("p (c i) t -> p c t i", i=4),
+                yg[:, :, cols].rearrange("p t (c i) -> p c t i", i=4),
+                th[u][:, :, inner].rearrange("p t (c i) -> p c t i", i=4),
                 ALU.mult,
             )
 
@@ -214,6 +236,7 @@ def tile_picked_twtjointbpagez_none_po_kernel(
         product(2)
         quantise(z_codes, z_scale, pieces[1], z_bf[1])
         quantise(z_codes, z_scale, pieces[2], z_bf[2])
+        w1_dealt.append(deal_w1("w1_late", 1, 3, ("z_bf2", "z_bf1")))
 
         pos = [sb("pos%d" % t, [P, WIDE], F32) for t in range(PACK)]
         h_rows = [sb("h%d" % t, [P, H], F32) for t in range(PACK)]
@@ -222,7 +245,7 @@ def tile_picked_twtjointbpagez_none_po_kernel(
             made = []
             for cols in (pieces if t == 0 else [whole]):
                 acc = bank()
-                mx(acc[:, cols], w1_dealt, w1_scale, t, z_codes, z_scale, cols)
+                mx(acc[:, cols], *w1_dealt[min(t, 1)], max(t - 1, 0), z_codes, z_scale, cols)
                 nc.scalar.activation(pos[t][:, cols], acc[:, cols], ACT.Relu)
                 made.append((h_rows[t][:, cols], acc[:, cols]))
             for dst, src in waiting:
@@ -267,8 +290,8 @@ def tile_picked_twtjointbpagez_none_po_kernel(
         round_page(PACK - 1, 3, nc.scalar.copy)
         for k in range(4):
             quantise(out_codes, out_scale, quarters[k], page_bf[k])
-            if k % 2 == 1:
-                cols = slice(quarters[k - 1].start, quarters[k].stop)
+            if k > 0:
+                cols = slice(0 if k == 1 else quarters[k].start, quarters[k].stop)
                 nc.sync.dma_start(words_view(out_1)[:, cols], out_codes[:, cols].bitcast(I32))
         for q in range(4):
             queue = nc.sync if q % 2 == 0 else nc.scalar

@@ -41,18 +41,12 @@ def tile_picked_twtjointbpagez_none_po_kernel(
             nc.sync.dma_start(tile[:], src)
             return tile
 
-        def load_scale_rows(queue, tile, src):
+        def load_scale_rows(queues, tile, src):
             for q in range(4):
-                queue.dma_start(tile[32 * q : 32 * q + 4, :].bitcast(I32), src[0, 4 * q : 4 * q + 4, :].bitcast(I32))
+                queues[q % len(queues)].dma_start(tile[32 * q : 32 * q + 4, :].bitcast(I32), src[0, 4 * q : 4 * q + 4, :].bitcast(I32))
 
         def words_view(src):
             return src[0].rearrange("p c r -> p (c r)").bitcast(I32)
-
-        def deal_words(dst, src):
-            nc.vector.tensor_copy(
-                dst[:].rearrange("p (t c i) -> p c t i", t=PACK, i=4),
-                src[:].rearrange("p (c i t) -> p c t i", t=PACK, i=4),
-            )
 
         def deal_bytes(dst, src):
             nc.vector.tensor_copy(
@@ -70,19 +64,21 @@ def tile_picked_twtjointbpagez_none_po_kernel(
         xs = sb("xs", [P, T], U8)
         nc.vector.memset(xs[:, : T // 2].bitcast(I32), 0)
         nc.gpsimd.memset(xs[:, T // 2 :].bitcast(I32), 0)
-        load_scale_rows(nc.sync, xs, x_scales)
+        load_scale_rows((nc.sync, nc.scalar), xs, x_scales)
         two_l = load_list("two_l", two)
         offs_l = load_list("offs_l", offs)
         n2_l = load_list("n2_l", n2)
         xw = sb("xw", [P, T], U32)
         nc.sync.dma_start(xw[:].bitcast(I32), words_view(x_words))
 
-        def load_weight_half(name, w, u):
-            raw = sb(name, [P, PACK, HALF], F32)
-            nc.sync.dma_start(raw[:], w.rearrange("(p j) c -> p j c", j=PACK)[:, :, HALF * u : HALF * (u + 1)])
+        pieces = [slice(0, 256), slice(256, 384), slice(384, 512)]
+
+        def load_weight_piece(name, w, cols):
+            raw = sb(name, [P, PACK, cols.stop - cols.start], F32)
+            nc.sync.dma_start(raw[:], w.rearrange("(p j) c -> p j c", j=PACK)[:, :, cols])
             return raw
 
-        wb_raw = [load_weight_half("wb_raw%d" % u, wb, u) for u in range(2)]
+        wb_raw = [load_weight_piece("wb_raw%d" % u, wb, cols) for u, cols in enumerate(pieces)]
         n1_l = load_list("n1_l", n1)
         wa_all = sb("wa_all", [P, PACK, H], F32)
         nc.sync.dma_start(wa_all[:], wa.rearrange("(p j) c -> p j c", j=PACK))
@@ -91,7 +87,7 @@ def tile_picked_twtjointbpagez_none_po_kernel(
         nc.gpsimd.memset(w1s[:].bitcast(I32), 0)
         w1w = sb("w1w", [P, N], U32)
         nc.sync.dma_start(w1w[:].bitcast(I32), words_view(w1_words))
-        load_scale_rows(nc.sync, w1s, w1_scales)
+        load_scale_rows((nc.sync,), w1s, w1_scales)
         gate = sb("gate", [P, PACK], F32)
         nc.sync.dma_start(gate[:], gt.rearrange("(p t) o -> p (t o)", t=PACK))
         n4_l = load_list("n4_l", n4)
@@ -108,23 +104,20 @@ def tile_picked_twtjointbpagez_none_po_kernel(
             return got
 
         def pick_words(name, lst, tag=None):
-            got = sb(name + "_got", [P, 16 * lst.shape[1]], U32, tag)
-            nc.vector.tensor_copy(got[:], xw[:].indirect(lst))
+            got = sb(name, [P, S], U32, tag)
+            nc.vector.tensor_copy(got[:].rearrange("p (t m) -> p m t", t=PACK), xw[:].indirect(lst[:]))
             return got
 
         bs_got = pick_bytes("bs", two_l, None)
         as_got = pick_bytes("as", offs_l, None)
         b_scale = sb("b_scale", [P, S], U8)
         deal_bytes(b_scale, bs_got)
-        bw_got = pick_words("bw", two_l[:])
-        aw_first = pick_words("aw0", offs_l[:, :16])
+        b_words = pick_words("b_words", two_l)
         a_scale = sb("a_scale", [P, S], U8)
         deal_bytes(a_scale, as_got)
-        b_words = sb("b_words", [P, S], U32)
-        deal_words(b_words, bw_got)
 
         def round_weight_half(name, raw):
-            grouped = sb(name, [P, HALF, PACK], BF16)
+            grouped = sb(name, [P, raw.shape[2], PACK], BF16)
             nc.scalar.activation(
                 grouped[:].rearrange("p (c i) j -> p c j i", i=4),
                 raw.rearrange("p j (c i) -> p c j i", i=4), ACT.Copy,
@@ -140,15 +133,9 @@ def tile_picked_twtjointbpagez_none_po_kernel(
         whole = slice(0, H)
         wb_codes = sb("wb_codes", [P, H], U32)
         wb_scale = sb("wb_scale", [P, H], U8)
-        for u in range(2):
-            quantise(wb_codes, wb_scale, halves[u], round_weight_half("wb_bf%d" % u, wb_raw[u][:]))
-        aw_second = pick_words("aw1", offs_l[:, 16:], "wb_bf1")
-        a_words = sb("a_words", [P, S], U32)
-        for u, got in enumerate((aw_first, aw_second)):
-            nc.vector.tensor_copy(
-                a_words[:].rearrange("p (t u c i) -> p u c t i", t=PACK, u=2, i=4)[:, u],
-                got[:].rearrange("p (c i t) -> p c t i", t=PACK, i=4),
-            )
+        for u, cols in enumerate(pieces):
+            quantise(wb_codes, wb_scale, cols, round_weight_half("wb_bf%d" % u, wb_raw[u][:]))
+        a_words = pick_words("a_words", offs_l, "wb_bf2")
 
         d_rows = [sb("d%d" % t, [P, WIDE], F32) for t in range(PACK)]
 
@@ -159,9 +146,9 @@ def tile_picked_twtjointbpagez_none_po_kernel(
 
         wa_codes = sb("wa_codes", [P, H], U32)
         wa_scale = sb("wa_scale", [P, H], U8)
-        for u in range(2):
+        for cols in pieces:
             for t in range(2):
-                project_d(t, halves[u])
+                project_d(t, cols)
         wa_bf = [round_weight_half("wa_bf%d" % u, wa_raw[u]) for u in range(2)]
         project_d(2, whole)
         project_d(3, whole)
@@ -194,7 +181,7 @@ def tile_picked_twtjointbpagez_none_po_kernel(
         seconds.extend([fetch_second(2), fetch_second(3)])
         diffs.append(fetch_diff(2, seconds[2], [whole]))
         diffs.append(fetch_diff(3, seconds[3], halves))
-        th = [sb("th0", [P, PACK, HALF], F32, "a_words"), sb("th1", [P, PACK, HALF], F32, "wa_codes")]
+        th = [sb("th0", [P, PACK, HALF], F32, "wa_scale"), sb("th1", [P, PACK, HALF], F32, "wa_codes")]
         for t in range(PACK):
             for u in range(2):
                 nc.scalar.activation(th[u][:, t, :], diffs[t][:, halves[u]], ACT.Tanh)
@@ -214,7 +201,6 @@ def tile_picked_twtjointbpagez_none_po_kernel(
 
         w1_dealt = [deal_w1("w1_early", 0, 1, (None, None))]
 
-        pieces = [slice(0, 256), slice(256, 384), slice(384, 512)]
         z_codes = sb("z_codes", [P, H], U32)
         z_scale = sb("z_scale", [P, H], U8)
         z_bf = [sb("z_bf%d" % k, [P, c.stop - c.start, PACK], BF16) for k, c in enumerate(pieces)]
@@ -256,8 +242,8 @@ def tile_picked_twtjointbpagez_none_po_kernel(
 
         minus = [sb("minus%d" % t, [P, H], F32) for t in range(PACK)]
         QUARTER = U // 4
-        quarters = [slice(QUARTER * k, QUARTER * (k + 1)) for k in range(4)]
-        page_bf = [sb("page_bf%d" % k, [P, QUARTER, PACK], BF16) for k in range(4)]
+        quarters = [slice(0, 256), slice(256, 512), slice(512, 768), slice(768, 896), slice(896, 1024)]
+        page_bf = [sb("page_bf%d" % k, [P, c.stop - c.start, PACK], BF16) for k, c in enumerate(quarters)]
         out_rows = out_0.rearrange("(p t) c -> p t c", t=PACK)
 
         def fetch_minus(t):
@@ -274,7 +260,7 @@ def tile_picked_twtjointbpagez_none_po_kernel(
         fetch_minus(1)
         for t in range(PACK - 1):
             put(t)
-            for k in range(4):
+            for k in range(5):
                 if t == PACK - 2 and k < 2:
                     nc.scalar.copy(page_bf[k][:, :, t:], pages[t][:, quarters[k]].unsqueeze(2).to_broadcast([P, QUARTER, 2]))
                 else:
@@ -288,10 +274,11 @@ def tile_picked_twtjointbpagez_none_po_kernel(
         round_page(PACK - 1, 1, nc.vector.tensor_copy)
         round_page(PACK - 1, 2, nc.scalar.copy)
         round_page(PACK - 1, 3, nc.scalar.copy)
-        for k in range(4):
+        round_page(PACK - 1, 4, nc.scalar.copy)
+        for k in range(5):
             quantise(out_codes, out_scale, quarters[k], page_bf[k])
-            if k > 0:
-                cols = slice(0 if k == 1 else quarters[k].start, quarters[k].stop)
+            if k in (1, 2, 4):
+                cols = slice(quarters[k if k == 2 else k - 1].start, quarters[k].stop)
                 nc.sync.dma_start(words_view(out_1)[:, cols], out_codes[:, cols].bitcast(I32))
         for q in range(4):
             queue = nc.sync if q % 2 == 0 else nc.scalar

@@ -93,10 +93,12 @@ def tile_picked_twtjointbpagez_none_po_kernel(
         n4_l = load_list("n4_l", n4)
         n3_l = load_list("n3_l", n3)
 
-        pages = [sb("page%d" % t, [P, U], F32) for t in range(PACK - 1)]
-        for page in pages:
+        def cleared_page(name, tag=None):
+            page = sb(name, [P, U], F32, tag)
             nc.vector.memset(page[:].bitcast(I32), 0)
-        pages.append(pages[0])
+            return page
+
+        pages = [cleared_page("page0"), cleared_page("page1")]
 
         def pick_bytes(name, lst, tag):
             got = sb(name + "_got", [P, S], U8, tag)
@@ -224,6 +226,7 @@ def tile_picked_twtjointbpagez_none_po_kernel(
         quantise(z_codes, z_scale, pieces[2], z_bf[2])
         w1_dealt.append(deal_w1("w1_late", 1, 3, ("z_bf2", "z_bf1")))
 
+        pages.extend([cleared_page("page2", "w1w"), pages[0]])
         pos = [sb("pos%d" % t, [P, WIDE], F32) for t in range(PACK)]
         h_rows = [sb("h%d" % t, [P, H], F32) for t in range(PACK)]
         waiting = []

from contextlib import ExitStack

import concourse.mybir as mybir

K, T, S, N, H, U = 512, 2048, 512, 512, 512, 1024
FLOPS = 2 * K * S * H * 2 + 2 * S * N * H

F32 = mybir.dt.float32
BF16 = mybir.dt.bfloat16
I32 = mybir.dt.int32
U32 = mybir.dt.uint32
U16 = mybir.dt.uint16
U8 = mybir.dt.uint8
FP8X4 = mybir.dt.float8_e4m3fn_x4
ALU = mybir.AluOpType
ACT = mybir.ActivationFunctionType

P = 128
PACK = 4
HALF = 256
WIDE = 1024


def tile_picked_twtjointbpagez_none_po_kernel(
    tc, x_words, x_scales, wa, wb, gt, w1_words, w1_scales, offs, two, n1, n2, n3, n4, out_0, out_1, out_2
):
    nc = tc.nc
    with ExitStack() as ctx:
        lists = ctx.enter_context(tc.tile_pool(name="lists", bufs=1))
        keep = ctx.enter_context(tc.tile_pool(name="keep", bufs=1))
        psum = ctx.enter_context(tc.psum_pool(name="psum", bufs=8))

        def sb(name, shape, dtype, tag=None):
            return keep.tile(shape, dtype, name=name, tag=tag or name, align_bytes=64)

        def bank():
            return psum.tile([P, 512], F32, name="bank")

        def load_list(name, src):
            tile = lists.tile([P, 32], U16, name=name)
            nc.sync.dma_start(tile[:], src)
            return tile

        def load_scale_rows(queues, tile, src):
            for q in range(4):
                queues[q % len(queues)].dma_start(tile[32 * q : 32 * q + 4, :].bitcast(I32), src[0, 4 * q : 4 * q + 4, :].bitcast(I32))

        def words_view(src):
            return src[0].rearrange("p c r -> p (c r)").bitcast(I32)

        def deal_bytes(dst, src):
            nc.vector.tensor_copy(
                dst[:].rearrange("p (t c i) -> p c t i", t=PACK, i=16),
                src[:].rearrange("p (c i t) -> p c t i", t=PACK, i=16),
            )

        def mx(acc, lhs, lhs_scale, t, rhs, rhs_scale, cols):
            rows = slice(P * t, P * (t + 1))
            nc.tensor.matmul_mx(
                out=acc, lhsT=lhs[:, rows].bitcast(FP8X4), lhsT_scale=lhs_scale[:, rows],
                rhs=rhs[:, cols].bitcast(FP8X4), rhs_scale=rhs_scale[:, cols], start=True, stop=True,
            )

        xs = sb("xs", [P, T], U8)
        nc.vector.memset(xs[:, : T // 2].bitcast(I32), 0)
        nc.gpsimd.memset(xs[:, T // 2 :].bitcast(I32), 0)
        load_scale_rows((nc.sync, nc.scalar), xs, x_scales)
        two_l = load_list("two_l", two)
        offs_l = load_list("offs_l", offs)
        n2_l = load_list("n2_l", n2)
        xw = sb("xw", [P, T], U32)
        nc.sync.dma_start(xw[:].bitcast(I32), words_view(x_words))

        pieces = [slice(0, 256), slice(256, 384), slice(384, 512)]

        def load_weight_piece(name, w, cols):
            raw = sb(name, [P, PACK, cols.stop - cols.start], F32)
            nc.sync.dma_start(raw[:], w.rearrange("(p j) c -> p j c", j=PACK)[:, :, cols])
            return raw

        wb_raw = [load_weight_piece("wb_raw%d" % u, wb, cols) for u, cols in enumerate(pieces)]
        n1_l = load_list("n1_l", n1)
        wa_all = sb("wa_all", [P, PACK, H], F32)
        nc.sync.dma_start(wa_all[:], wa.rearrange("(p j) c -> p j c", j=PACK))
        wa_raw = [wa_all[:, :, HALF * u : HALF * (u + 1)] for u in range(2)]
        w1s = sb("w1s", [P, N], U8)
        nc.gpsimd.memset(w1s[:].bitcast(I32), 0)
        w1w = sb("w1w", [P, N], U32)
        nc.sync.dma_start(w1w[:].bitcast(I32), words_view(w1_words))
        load_scale_rows((nc.sync,), w1s, w1_scales)
        gate = sb("gate", [P, PACK], F32)
        nc.sync.dma_start(gate[:], gt.rearrange("(p t) o -> p (t o)", t=PACK))
        n4_l = load_list("n4_l", n4)
        n3_l = load_list("n3_l", n3)

        def cleared_page(name, tag=None):
            page = sb(name, [P, U], F32, tag)
            nc.vector.memset(page[:].bitcast(I32), 0)
            return page

        pages = [cleared_page("page0"), cleared_page("page1")]

        def pick_bytes(name, lst, tag):
            got = sb(name + "_got", [P, S], U8, tag)
            nc.vector.tensor_copy(got[:], xs[:].indirect(lst[:]))
            return got

        def pick_words(name, lst, tag=None):
            got = sb(name, [P, S], U32, tag)
            nc.vector.tensor_copy(got[:].rearrange("p (t m) -> p m t", t=PACK), xw[:].indirect(lst[:]))
            return got

        bs_got = pick_bytes("bs", two_l, None)
        as_got = pick_bytes("as", offs_l, None)
        b_scale = sb("b_scale", [P, S], U8)
        deal_bytes(b_scale, bs_got)
        b_words = pick_words("b_words", two_l)
        a_scale = sb("a_scale", [P, S], U8)
        deal_bytes(a_scale, as_got)

        def round_weight_half(name, raw):
            grouped = sb(name, [P, raw.shape[2], PACK], BF16)
            nc.scalar.activation(
                grouped[:].rearrange("p (c i) j -> p c j i", i=4),
                raw.rearrange("p j (c i) -> p c j i", i=4), ACT.Copy,
            )
            return grouped

        def quantise(codes, scales, cols, grouped):
            nc.vector.quantize_mx(
                out=codes[:, cols].bitcast(FP8X4), scales=scales[:, cols], in_=grouped[:].rearrange("p c j -> p (c j)")
            )

        halves = [slice(0, HALF), slice(HALF, 2 * HALF)]
        whole = slice(0, H)
        wb_codes = sb("wb_codes", [P, H], U32)
        wb_scale = sb("wb_scale", [P, H], U8)
        for u, cols in enumerate(pieces):
            quantise(wb_codes, wb_scale, cols, round_weight_half("wb_bf%d" % u, wb_raw[u][:]))
        a_words = pick_words("a_words", offs_l, "wb_bf2")

        d_rows = [sb("d%d" % t, [P, WIDE], F32) for t in range(PACK)]

        def project_d(t, cols):
            acc = bank()
            mx(acc[:, cols], b_words, b_scale, t, wb_codes, wb_scale, cols)
            nc.scalar.copy(d_rows[t][:, cols], acc[:, cols])

        wa_codes = sb("wa_codes", [P, H], U32)
        wa_scale = sb("wa_scale", [P, H], U8)
        for cols in pieces:
            for t in range(2):
                project_d(t, cols)
        wa_bf = [round_weight_half("wa_bf%d" % u, wa_raw[u]) for u in range(2)]
        project_d(2, whole)
        project_d(3, whole)

        yg = sb("yg", [P, PACK, H], F32)

        def fetch_second(t):
            second = sb("second%d" % t, [P, H], F32)
            nc.vector.tensor_copy(second[:], d_rows[t][:].indirect(n2_l[:]))
            return second

        def fetch_diff(t, second, parts, tag=None):
            diff = sb("diff%d" % t, [P, H], F32, tag)
            for cols in parts:
                nc.vector.tensor_tensor(
                    diff[:, cols], d_rows[t][:].indirect(n1_l[:, cols.start // 16 : cols.stop // 16]),
                    second[:, cols], ALU.subtract,
                )
            return diff

        seconds = [fetch_second(0), fetch_second(1)]
        diffs = [fetch_diff(0, seconds[0], [whole])]
        for u in range(2):
            quantise(wa_codes, wa_scale, halves[u], wa_bf[u])
        for t in range(PACK):
            acc = bank()
            mx(acc[:], a_words, a_scale, t, wa_codes, wa_scale, whole)
            nc.scalar.activation(yg[:, t, :], acc[:], ACT.Copy, scale=gate[:, t : t + 1])
        diffs.append(fetch_diff(1, seconds[1], [whole], "wa_bf1"))
        seconds.extend([fetch_second(2), fetch_second(3)])
        diffs.append(fetch_diff(2, seconds[2], [whole]))
        diffs.append(fetch_diff(3, seconds[3], halves))
        th = [sb("th0", [P, PACK, HALF], F32, "wa_scale"), sb("th1", [P, PACK, HALF], F32, "wa_codes")]
        for t in range(PACK):
            for u in range(2):
                nc.scalar.activation(th[u][:, t, :], diffs[t][:, halves[u]], ACT.Tanh)

        def deal_w1(name, first, count, tags):
            words = sb(name + "_words", [P, count * P], U32, tags[0])
            scale = sb(name + "_scale", [P, count * P], U8, tags[1])
            nc.vector.tensor_copy(
                words[:].rearrange("p (t c i) -> p c t i", t=count, i=4),
                w1w[:].rearrange("p (c i t) -> p c t i", t=PACK, i=4)[:, :, first : first + count, :],
            )
            nc.vector.tensor_copy(
                scale[:].rearrange("p (t c i) -> p c t i", t=count, i=16),
                w1s[:].rearrange("p (c i t) -> p c t i", t=PACK, i=16)[:, :, first : first + count, :],
            )
            return words, scale

        w1_dealt = [deal_w1("w1_early", 0, 1, (None, None))]

        z_codes = sb("z_codes", [P, H], U32)
        z_scale = sb("z_scale", [P, H], U8)
        z_bf = [sb("z_bf%d" % k, [P, c.stop - c.start, PACK], BF16) for k, c in enumerate(pieces)]

        def product(k):
            cols = pieces[k]
            u = cols.start // HALF
            inner = slice(cols.start - HALF * u, cols.stop - HALF * u)
            nc.vector.tensor_tensor(
                z_bf[k][:].rearrange("p (c i) t -> p c t i", i=4),
                yg[:, :, cols].rearrange("p t (c i) -> p c t i", i=4),
                th[u][:, :, inner].rearrange("p t (c i) -> p c t i", i=4),
                ALU.mult,
            )

        product(0)
        product(1)
        quantise(z_codes, z_scale, pieces[0], z_bf[0])
        product(2)
        quantise(z_codes, z_scale, pieces[1], z_bf[1])
        quantise(z_codes, z_scale, pieces[2], z_bf[2])
        w1_dealt.append(deal_w1("w1_late", 1, 3, ("z_bf2", "z_bf1")))

        pages.extend([cleared_page("page2", "w1w"), pages[0]])
        pos = [sb("pos%d" % t, [P, WIDE], F32) for t in range(PACK)]
        h_rows = [sb("h%d" % t, [P, H], F32) for t in range(PACK)]
        waiting = []
        for t in range(PACK):
            made = []
            for cols in (pieces if t == 0 else [whole]):
                acc = bank()
                mx(acc[:, cols], *w1_dealt[min(t, 1)], max(t - 1, 0), z_codes, z_scale, cols)
                nc.scalar.activation(pos[t][:, cols], acc[:, cols], ACT.Relu)
                made.append((h_rows[t][:, cols], acc[:, cols]))
            for dst, src in waiting:
                nc.scalar.copy(dst, src)
            waiting = made
        for dst, src in waiting:
            nc.scalar.copy(dst, src)

        minus = [sb("minus%d" % t, [P, H], F32) for t in range(PACK)]
        QUARTER = U // 4
        quarters = [slice(0, 256), slice(256, 512), slice(512, 768), slice(768, 896), slice(896, 1024)]
        page_bf = [sb("page_bf%d" % k, [P, c.stop - c.start, PACK], BF16) for k, c in enumerate(quarters)]
        out_rows = out_0.rearrange("(p t) c -> p t c", t=PACK)

        def fetch_minus(t):
            nc.vector.tensor_scalar(minus[t][:], pos[t][:].indirect(n4_l[:]), -1.0, 0.0, ALU.mult, ALU.add)

        def put(t):
            nc.vector.tensor_tensor(pages[t][:].indirect(n3_l[:]), h_rows[t][:], minus[t][:], ALU.add)
            nc.sync.dma_start(out_rows[:, t, :], pages[t][:])

        def round_page(t, k, copy):
            copy(page_bf[k][:, :, t], pages[t][:, quarters[k]])

        fetch_minus(0)
        fetch_minus(1)
        for t in range(PACK - 1):
            put(t)
            for k in range(5):
                if t == PACK - 2 and k < 2:
                    nc.scalar.copy(page_bf[k][:, :, t:], pages[t][:, quarters[k]].unsqueeze(2).to_broadcast([P, QUARTER, 2]))
                else:
                    round_page(t, k, nc.scalar.copy)
            if t + 2 < PACK:
                fetch_minus(t + 2)
        put(PACK - 1)
        out_codes = sb("out_codes", [P, U], U32)
        out_scale = sb("out_scale", [P, U], U8)
        round_page(PACK - 1, 0, nc.vector.tensor_copy)
        round_page(PACK - 1, 1, nc.vector.tensor_copy)
        round_page(PACK - 1, 2, nc.scalar.copy)
        round_page(PACK - 1, 3, nc.scalar.copy)
        round_page(PACK - 1, 4, nc.scalar.copy)
        for k in range(5):
            quantise(out_codes, out_scale, quarters[k], page_bf[k])
            if k in (1, 2, 4):
                cols = slice(quarters[k if k == 2 else k - 1].start, quarters[k].stop)
                nc.sync.dma_start(words_view(out_1)[:, cols], out_codes[:, cols].bitcast(I32))
        for q in range(4):
            queue = nc.sync if q % 2 == 0 else nc.scalar
            queue.dma_start(out_2[0, 4 * q : 4 * q + 4, :].bitcast(I32), out_scale[32 * q : 32 * q + 4, :].bitcast(I32))
